import numpy as np
import ml_dtypes


def mxq(x, axis, fmt="e4m3"):
    dtype, down = {"e4m3": (ml_dtypes.float8_e4m3fn, 7), "e5m2": (ml_dtypes.float8_e5m2, 14)}[fmt]
    v = np.moveaxis(np.asarray(x, np.float32).astype(ml_dtypes.bfloat16).astype(np.float64), axis, -1)
    blocks = v.reshape(v.shape[:-1] + (-1, 32))
    amax = np.abs(blocks).max(-1, keepdims=True)
    byte = np.maximum(np.where(amax > 0, np.frexp(amax)[1] - 1 + 127, 0) - down, 1)
    scale = np.exp2(byte - 127.0)
    codes = (blocks / scale).astype(np.float32).astype(dtype).astype(np.float64)
    return np.moveaxis((codes * scale).reshape(v.shape), -1, axis)


WIDE = False


def mx_kscale(k):
    if not WIDE:
        return np.ones(k)
    levels = np.array([10, -10, 5, -5, 0])
    if k % 512:
        return np.exp2(np.random.permutation(np.resize(levels, k // 32))).repeat(32)
    a = np.empty((k // 512, 16))
    for p in range(k // 512):
        a[p, :8] = np.random.permutation(np.resize(levels, 8))
        for g in range(8):
            far = levels[np.abs(levels - a[p, g]) >= 10]
            a[p, g + 8] = far[np.random.randint(len(far))]
    return np.exp2(a.ravel()).repeat(32)


def f64(x):
    return np.asarray(x).astype(np.float64)


def striped(idx):
    return np.tile(idx.reshape(-1, 16).T, (8, 1)).astype(np.uint16)


def unstriped(offs):
    return offs[:16].T.reshape(-1).astype(np.int64)


def striped8(idx):
    return np.concatenate([v.reshape(-1, 16).T for v in idx]).astype(np.uint16)


def unstriped8(offs):
    return np.stack([offs[16 * g:16 * g + 16].T.reshape(-1) for g in range(8)]).astype(np.int64)


E2M1 = np.array([0.0, 0.5, 1.0, 1.5, 2.0, 3.0, 4.0, 6.0, -0.0, -0.5, -1.0, -1.5, -2.0, -3.0, -4.0, -6.0])


def pack_weight(w, fmt):
    k, n = w.shape
    w = f64(np.asarray(w, np.float32).astype(ml_dtypes.bfloat16)).reshape(k // 32, 32, n)
    amax = np.abs(w).max(1)
    if fmt == "e4m3":
        byte = np.frexp(amax)[1] - 1 + 127 - 7
    else:
        mant, ex = np.frexp(amax / 6.0)
        byte = np.where(mant > 0.5, ex, ex - 1) + 127
    byte = np.clip(np.where(amax > 0, byte, 1), 1, 254)
    scaled = (w * np.exp2(127.0 - byte)[:, None, :]).reshape(k, n).astype(np.float32)
    by_word = np.ascontiguousarray(scaled.reshape(k // 512, 128, 4, n).transpose(0, 1, 3, 2))
    if fmt == "e4m3":
        words = by_word.astype(ml_dtypes.float8_e4m3fn).view(np.uint8)
    else:
        c = by_word.astype(ml_dtypes.float4_e2m1fn).view(np.uint8) & 0xF
        words = (c[..., 0::2] | (c[..., 1::2] << 4)).reshape(k // 512, 128, 2 * n)
    return np.ascontiguousarray(words), np.ascontiguousarray(byte.astype(np.uint8).reshape(k // 512, 16, n))


def unpack_weight(words, scales, fmt):
    g, _, n = scales.shape
    words = np.ascontiguousarray(words).reshape(g, 128, n, -1)
    if fmt == "e4m3":
        vals = words.view(ml_dtypes.float8_e4m3fn).astype(np.float64)
    else:
        nib = np.empty((g, 128, n, 4), np.uint8)
        nib[..., 0::2] = words & 0xF
        nib[..., 1::2] = words >> 4
        vals = E2M1[nib]
    vals = vals * np.repeat(np.exp2(scales.astype(np.float64) - 127.0), 8, axis=1)[..., None]
    return vals.transpose(0, 1, 3, 2).reshape(g * 512, n)


def pack_table(v):
    words, scales = pack_weight(v, "e4m3")
    return np.concatenate([words.reshape(words.shape[0], -1), scales.reshape(scales.shape[0], -1)], axis=1)


def unpack_table(tab):
    g, t = tab.shape[0], tab.shape[1] // 528
    return unpack_weight(tab[:, :512 * t].reshape(g, 128, t, 4), tab[:, 512 * t:].reshape(g, 16, t), "e4m3")


def silu(v):
    return v / (1.0 + np.exp(-np.maximum(v, -700.0)))


K, L, M, T, S = 512, 512, 256, 2048, 512


def setup_inputs():
    n = np.random.standard_normal
    s1 = mx_kscale(K)[:, None]
    s2 = mx_kscale(L)[:, None]
    p_w4 = pack_weight(n((K, M)) / np.sqrt(K) / s1, "e2m1")
    return {
        "xT": (n((K, T)) * s1).astype(np.float32),
        "w4_words": p_w4[0],
        "w4_scales": p_w4[1],
        "tab": pack_table(n((L, T)) * s2),
        "u": (n((L, M)) / np.sqrt(L) / s2).astype(np.float32),
        "wgt": np.repeat(np.random.uniform(0.5, 2.0, (8, S)), 16, axis=0).astype(np.float32),
        "b": (0.3 * n(256)).astype(np.float32),
        "offs": striped(np.random.permutation(T)[:S]),
        "offs2": striped8(np.stack([np.random.permutation(T)[:S] for _ in range(8)])),
    }


def reference(xT, w4_words, w4_scales, tab, u, wgt, b, offs, offs2):
    idx2 = unstriped8(offs2)
    group = np.arange(K) % 512 // 64
    xg = f64(wgt)[np.arange(K) // 4 % 128] * f64(xT)[np.arange(K)[:, None], idx2[group]]
    xT_ = mxq(xg, 0, "e4m3")
    w4_ = unpack_weight(w4_words, w4_scales, "e2m1")
    tab_ = unpack_table(tab)[:, unstriped(offs)]
    u_ = mxq(f64(u), 0, "e4m3")
    y = w4_.T @ xT_ + u_.T @ tab_
    return silu(y + f64(b)[:, None])

@@ -1,0 +1,166 @@
+from contextlib import ExitStack
+
+import concourse.mybir as mybir
+
+K, L, M, T, S = 512, 512, 256, 2048, 512
+FLOPS = 2 * (K + L) * M * S
+
+F32 = mybir.dt.float32
+BF16 = mybir.dt.bfloat16
+I32 = mybir.dt.int32
+U32 = mybir.dt.uint32
+U16 = mybir.dt.uint16
+U8 = mybir.dt.uint8
+FP8X4 = mybir.dt.float8_e4m3fn_x4
+FP4X4 = mybir.dt.float4_e2m1fn_x4
+MULT = mybir.AluOpType.mult
+SILU = mybir.ActivationFunctionType.Silu
+
+P = 128
+PACK = 4
+HALF = S // 2
+LIST_HALF = HALF // 16
+M_TILES = M // P
+
+
+def tile_list_htab_silu_kernel(tc, xT, w4_words, w4_scales, tab, u, wgt, b, offs, offs2, out):
+    nc = tc.nc
+    with ExitStack() as ctx:
+        keep = ctx.enter_context(tc.tile_pool(name="keep", bufs=1))
+        psum = ctx.enter_context(tc.psum_pool(name="psum", bufs=1))
+
+        head_lists = keep.tile([P, S // 16], U16, name="head_lists")
+        table_list = keep.tile([P, S // 16], U16, name="table_list")
+        planes = [keep.tile([P, T], F32, name="plane%d" % i) for i in range(2)]
+        w4_codes = keep.tile([P, 2 * M], U8, name="w4_codes", align_bytes=64)
+        w4_plane = keep.tile([P, M], U8, name="w4_plane", align_bytes=64)
+        table_scales = keep.tile([P, T], U8, name="table_scales", tag="scales_then_words")
+        folded = keep.tile([P, 32], F32, name="folded", align_bytes=64, tag="folded_then_plane2")
+        bias = keep.tile([P, M_TILES], F32, name="bias")
+
+        nc.vector.memset(table_scales[:].bitcast(I32), 0)
+        nc.gpsimd.memset(w4_plane[:].bitcast(I32), 0)
+
+        x_planes = xT.rearrange("(p i) t -> i p t", i=PACK)
+        nc.sync.dma_start(folded[:], wgt[0:P:16, :].rearrange("g (c j) -> g c j", j=32))
+        nc.sync.dma_start(head_lists[:], offs2)
+        nc.sync.dma_start(planes[0][:], x_planes[0])
+        nc.sync.dma_start(table_list[:], offs)
+        nc.sync.dma_start(w4_codes[:].bitcast(I32), w4_words[0].bitcast(I32))
+        nc.sync.dma_start(planes[1][:], x_planes[1])
+
+        nc.scalar.dma_start(
+            table_scales[:].bitcast(I32)[0:P:8, :],
+            tab[0, 512 * T : 528 * T].rearrange("(q t) -> q t", q=16).bitcast(I32),
+        )
+        for q in range(4):
+            nc.gpsimd.dma_start(
+                w4_plane[:].bitcast(I32)[32 * q : 32 * q + 4, :],
+                w4_scales[0, 4 * q : 4 * q + 4, :].bitcast(I32),
+            )
+
+        with nc.allow_non_contiguous_dma(reason="one bias value for each partition and tile of rows"):
+            nc.gpsimd.dma_start(bias[:], b.rearrange("(m p) -> p m", p=P))
+
+        turned = keep.tile([P, 32], F32, name="turned", align_bytes=64, tag="turned_then_plane3")
+        spread = keep.tile([P, S], F32, name="spread", align_bytes=64, tag="spread_then_u")
+        weights = keep.tile([P, S], F32, name="weights", align_bytes=64)
+        nc.vector.transpose(turned[:], folded[:])
+        nc.vector.tensor_copy(
+            spread[:].rearrange("p (c g r) -> p c g r", g=2, r=16),
+            turned[:].rearrange("p (g c) -> p c g", g=2).unsqueeze(3).to_broadcast([P, 16, 2, 16]),
+        )
+        nc.vector.transpose(weights[:], spread[:])
+
+        planes.append(keep.tile([P, T], F32, name="plane2", align_bytes=64, tag="folded_then_plane2"))
+        planes.append(keep.tile([P, T], F32, name="plane3", align_bytes=64, tag="turned_then_plane3"))
+        u_rows = keep.tile([P, PACK, M], F32, name="u_rows", align_bytes=64, tag="spread_then_u")
+        for i in range(2, PACK):
+            nc.sync.dma_start(planes[i][:], x_planes[i])
+        nc.sync.dma_start(u_rows[:], u.rearrange("(p i) n -> p i n", i=PACK))
+
+        cols = [slice(h * HALF, (h + 1) * HALF) for h in range(2)]
+        list_cols = [slice(h * LIST_HALF, (h + 1) * LIST_HALF) for h in range(2)]
+        woven = [keep.tile([P, HALF, PACK], BF16, name="woven%d" % h, align_bytes=64) for h in range(2)]
+
+        low = keep.tile([P, 2, S], F32, name="low")
+        for i in range(2):
+            nc.vector.tensor_tensor(low[:, i, :], planes[i][:].indirect(head_lists[:]), weights[:], MULT)
+        for h in range(2):
+            nc.scalar.copy(woven[h][:, :, 0:2], low[:, :, cols[h]].rearrange("p i s -> p s i"))
+
+        picked_scales = keep.tile([P, S], U8, name="picked_scales")
+        table_plane = keep.tile([P, S], U8, name="table_plane", align_bytes=64)
+        nc.vector.tensor_copy(picked_scales[:], table_scales[:].indirect(table_list[:]))
+        nc.vector.tensor_copy(table_plane[:].bitcast(I32), picked_scales[:].bitcast(I32))
+        table_words = keep.tile([P, T], I32, name="table_words", tag="scales_then_words")
+        nc.sync.dma_start(table_words[:], tab[0, 0 : 512 * T].rearrange("(p c) -> p c", p=P).bitcast(I32))
+        for r in range(1, 4):
+            nc.gpsimd.dma_start(
+                table_plane[:].bitcast(I32)[r:P:32, :],
+                picked_scales[:].bitcast(I32)[8 * r : P : 32, :],
+            )
+
+        high = [keep.tile([P, 2, HALF], F32, name="high%d" % h) for h in range(2)]
+        for i in range(2):
+            for h in range(2):
+                nc.vector.tensor_tensor(
+                    high[h][:, i, :], planes[2 + i][:].indirect(head_lists[:, list_cols[h]]), weights[:, cols[h]], MULT
+                )
+        nc.scalar.copy(woven[0][:, :, 2:4], high[0][:].rearrange("p i s -> p s i"))
+        nc.vector.tensor_copy(woven[1][:, :, 2:4], high[1][:].rearrange("p i s -> p s i"))
+
+        x_codes = [keep.tile([P, HALF], U32, name="x_codes%d" % h, align_bytes=64) for h in range(2)]
+        x_scales = [keep.tile([P, HALF], U8, name="x_scales%d" % h, align_bytes=64) for h in range(2)]
+        for h in range(2):
+            nc.vector.quantize_mx(
+                out=x_codes[h][:].bitcast(FP8X4), scales=x_scales[h][:], in_=woven[h][:].rearrange("p s i -> p (s i)")
+            )
+
+        banks = [[psum.tile([P, HALF], F32, name="bank%d%d" % (m, h)) for h in range(2)] for m in range(M_TILES)]
+        for h in range(2):
+            for m in range(M_TILES):
+                for n in range(HALF // P):
+                    nc.tensor.matmul_mx(
+                        out=banks[m][h][:, n * P : (n + 1) * P],
+                        lhsT=w4_codes[:, 2 * m * P : 2 * (m + 1) * P].bitcast(FP4X4),
+                        lhsT_scale=w4_plane[:, m * P : (m + 1) * P],
+                        rhs=x_codes[h][:, n * P : (n + 1) * P].bitcast(FP8X4),
+                        rhs_scale=x_scales[h][:, n * P : (n + 1) * P],
+                        start=(n == 0),
+                        stop=False,
+                    )
+
+        u_woven = [keep.tile([P, P, PACK], BF16, name="u_woven%d" % m, align_bytes=64) for m in range(M_TILES)]
+        u_codes = [keep.tile([P, P], U32, name="u_codes%d" % m, align_bytes=64) for m in range(M_TILES)]
+        u_scales = [keep.tile([P, P], U8, name="u_scales%d" % m, align_bytes=64) for m in range(M_TILES)]
+        u_views = [
+            (
+                u_woven[m][:].rearrange("p (c j) i -> p c i j", j=4),
+                u_rows[:, :, m * P : (m + 1) * P].rearrange("p i (c j) -> p c i j", j=4),
+            )
+            for m in range(M_TILES)
+        ]
+        nc.scalar.copy(*u_views[0])
+        nc.vector.tensor_copy(*u_views[1])
+        for m in range(M_TILES):
+            nc.vector.quantize_mx(
+                out=u_codes[m][:].bitcast(FP8X4), scales=u_scales[m][:], in_=u_woven[m][:].rearrange("p n i -> p (n i)")
+            )
+
+        for h in range(2):
+            picked_words = keep.tile([P, HALF], U32, name="picked_words%d" % h, align_bytes=64)
+            nc.vector.tensor_copy(picked_words[:], table_words[:].bitcast(U32).indirect(table_list[:, list_cols[h]]))
+            for m in range(M_TILES):
+                nc.tensor.matmul_mx(
+                    out=banks[m][h][:],
+                    lhsT=u_codes[m][:].bitcast(FP8X4),
+                    lhsT_scale=u_scales[m][:],
+                    rhs=picked_words[:].bitcast(FP8X4),
+                    rhs_scale=table_plane[:, cols[h]],
+                    start=False,
+                    stop=True,
+                )
+                result = keep.tile([P, HALF], F32, name="result%d%d" % (m, h))
+                nc.scalar.activation(result[:], banks[m][h][:], SILU, bias=bias[:, m : m + 1])
+                nc.sync.dma_start(out[m * P : (m + 1) * P, cols[h]], result[:])

@@ -33,18 +33,21 @@ def tile_list_htab_silu_kernel(tc, xT, w4_words, w4_scales, tab, u, wgt, b, offs
         table_list = keep.tile([P, S // 16], U16, name="table_list")
         planes = [keep.tile([P, T], F32, name="plane%d" % i) for i in range(2)]
         w4_codes = keep.tile([P, 2 * M], U8, name="w4_codes", align_bytes=64)
-        w4_plane = keep.tile([P, M], U8, name="w4_plane", align_bytes=64)
+        scale_planes = keep.tile([P, S + M], U8, name="scale_planes", align_bytes=64)
+        bias_rows = keep.tile([P, P], F32, name="bias_rows", align_bytes=64)
         table_scales = keep.tile([P, T], U8, name="table_scales", tag="scales_then_words")
         folded = keep.tile([P, 32], F32, name="folded", align_bytes=64, tag="folded_then_plane2")
-        bias = keep.tile([P, M_TILES], F32, name="bias")
+        bias = keep.tile([P, P], F32, name="bias", align_bytes=64)
+        warm = keep.tile([P, 1], F32, name="warm")
 
         nc.vector.memset(table_scales[:].bitcast(I32), 0)
-        nc.gpsimd.memset(w4_plane[:].bitcast(I32), 0)
+        nc.vector.memset(scale_planes[:].bitcast(I32)[:, S // 4 :], 0)
+        nc.vector.memset(bias_rows[:], 0.0)
 
         x_planes = xT.rearrange("(p i) t -> i p t", i=PACK)
         nc.sync.dma_start(folded[:], wgt[0:P:16, :].rearrange("g (c j) -> g c j", j=32))
-        nc.sync.dma_start(head_lists[:], offs2)
         nc.sync.dma_start(planes[0][:], x_planes[0])
+        nc.sync.dma_start(head_lists[:], offs2)
         nc.sync.dma_start(table_list[:], offs)
         nc.sync.dma_start(w4_codes[:].bitcast(I32), w4_words[0].bitcast(I32))
         nc.sync.dma_start(planes[1][:], x_planes[1])
@@ -53,14 +56,11 @@ def tile_list_htab_silu_kernel(tc, xT, w4_words, w4_scales, tab, u, wgt, b, offs
             table_scales[:].bitcast(I32)[0:P:8, :],
             tab[0, 512 * T : 528 * T].rearrange("(q t) -> q t", q=16).bitcast(I32),
         )
-        for q in range(4):
-            nc.gpsimd.dma_start(
-                w4_plane[:].bitcast(I32)[32 * q : 32 * q + 4, :],
-                w4_scales[0, 4 * q : 4 * q + 4, :].bitcast(I32),
-            )
-
-        with nc.allow_non_contiguous_dma(reason="one bias value for each partition and tile of rows"):
-            nc.gpsimd.dma_start(bias[:], b.rearrange("(m p) -> p m", p=P))
+        nc.scalar.dma_start(scale_planes[:].bitcast(I32)[0:P:8, S // 4 :], w4_scales[0].bitcast(I32))
+        nc.scalar.dma_start(
+            bias_rows[0:P:32, 0 : 32 * M_TILES].rearrange("q (m r) -> q m r", r=32),
+            b.rearrange("(m q r) -> q m r", q=4, r=32),
+        )
 
         turned = keep.tile([P, 32], F32, name="turned", align_bytes=64, tag="turned_then_plane3")
         spread = keep.tile([P, S], F32, name="spread", align_bytes=64, tag="spread_then_u")
@@ -71,6 +71,7 @@ def tile_list_htab_silu_kernel(tc, xT, w4_words, w4_scales, tab, u, wgt, b, offs
             turned[:].rearrange("p (g c) -> p c g", g=2).unsqueeze(3).to_broadcast([P, 16, 2, 16]),
         )
         nc.vector.transpose(weights[:], spread[:])
+        nc.scalar.activation(warm[:], weights[:, 0:1], SILU)
 
         planes.append(keep.tile([P, T], F32, name="plane2", align_bytes=64, tag="folded_then_plane2"))
         planes.append(keep.tile([P, T], F32, name="plane3", align_bytes=64, tag="turned_then_plane3"))
@@ -90,15 +91,15 @@ def tile_list_htab_silu_kernel(tc, xT, w4_words, w4_scales, tab, u, wgt, b, offs
             nc.scalar.copy(woven[h][:, :, 0:2], low[:, :, cols[h]].rearrange("p i s -> p s i"))
 
         picked_scales = keep.tile([P, S], U8, name="picked_scales")
-        table_plane = keep.tile([P, S], U8, name="table_plane", align_bytes=64)
         nc.vector.tensor_copy(picked_scales[:], table_scales[:].indirect(table_list[:]))
-        nc.vector.tensor_copy(table_plane[:].bitcast(I32), picked_scales[:].bitcast(I32))
+        nc.vector.tensor_copy(scale_planes[:].bitcast(I32)[:, : S // 4], picked_scales[:].bitcast(I32))
+        nc.vector.transpose(bias[:], bias_rows[:])
         table_words = keep.tile([P, T], I32, name="table_words", tag="scales_then_words")
         nc.sync.dma_start(table_words[:], tab[0, 0 : 512 * T].rearrange("(p c) -> p c", p=P).bitcast(I32))
         for r in range(1, 4):
-            nc.gpsimd.dma_start(
-                table_plane[:].bitcast(I32)[r:P:32, :],
-                picked_scales[:].bitcast(I32)[8 * r : P : 32, :],
+            nc.scalar.dma_start(
+                scale_planes[:].bitcast(I32)[r:P:32, :],
+                scale_planes[:].bitcast(I32)[8 * r : P : 32, :],
             )
 
         high = [keep.tile([P, 2, HALF], F32, name="high%d" % h) for h in range(2)]
@@ -124,7 +125,7 @@ def tile_list_htab_silu_kernel(tc, xT, w4_words, w4_scales, tab, u, wgt, b, offs
                     nc.tensor.matmul_mx(
                         out=banks[m][h][:, n * P : (n + 1) * P],
                         lhsT=w4_codes[:, 2 * m * P : 2 * (m + 1) * P].bitcast(FP4X4),
-                        lhsT_scale=w4_plane[:, m * P : (m + 1) * P],
+                        lhsT_scale=scale_planes[:, S + m * P : S + (m + 1) * P],
                         rhs=x_codes[h][:, n * P : (n + 1) * P].bitcast(FP8X4),
                         rhs_scale=x_scales[h][:, n * P : (n + 1) * P],
                         start=(n == 0),
@@ -157,10 +158,10 @@ def tile_list_htab_silu_kernel(tc, xT, w4_words, w4_scales, tab, u, wgt, b, offs
                     lhsT=u_codes[m][:].bitcast(FP8X4),
                     lhsT_scale=u_scales[m][:],
                     rhs=picked_words[:].bitcast(FP8X4),
-                    rhs_scale=table_plane[:, cols[h]],
+                    rhs_scale=scale_planes[:, cols[h]],
                     start=False,
                     stop=True,
                 )
                 result = keep.tile([P, HALF], F32, name="result%d%d" % (m, h))
-                nc.scalar.activation(result[:], banks[m][h][:], SILU, bias=bias[:, m : m + 1])
+                nc.scalar.activation(result[:], banks[m][h][:], SILU, bias=bias[:, 32 * m : 32 * m + 1])
                 nc.sync.dma_start(out[m * P : (m + 1) * P, cols[h]], result[:])

@@ -31,13 +31,14 @@ def tile_list_htab_silu_kernel(tc, xT, w4_words, w4_scales, tab, u, wgt, b, offs
 
         head_lists = keep.tile([P, S // 16], U16, name="head_lists")
         table_list = keep.tile([P, S // 16], U16, name="table_list")
-        planes = [keep.tile([P, T], F32, name="plane%d" % i) for i in range(2)]
-        w4_codes = keep.tile([P, 2 * M], U8, name="w4_codes", align_bytes=64)
+        planes = [
+            keep.tile([P, T], F32, name="plane0", align_bytes=64, tag="plane0_then_bias"),
+            keep.tile([P, T], F32, name="plane1"),
+        ]
         scale_planes = keep.tile([P, S + M], U8, name="scale_planes", align_bytes=64)
         bias_rows = keep.tile([P, P], F32, name="bias_rows", align_bytes=64)
-        table_scales = keep.tile([P, T], U8, name="table_scales", tag="scales_then_words")
+        table_scales = keep.tile([P, T], U8, name="table_scales", align_bytes=64, tag="scales_then_w4")
         folded = keep.tile([P, 32], F32, name="folded", align_bytes=64, tag="folded_then_plane2")
-        bias = keep.tile([P, P], F32, name="bias", align_bytes=64)
         warm = keep.tile([P, 1], F32, name="warm")
 
         nc.vector.memset(table_scales[:].bitcast(I32), 0)
@@ -49,7 +50,6 @@ def tile_list_htab_silu_kernel(tc, xT, w4_words, w4_scales, tab, u, wgt, b, offs
         nc.sync.dma_start(planes[0][:], x_planes[0])
         nc.sync.dma_start(head_lists[:], offs2)
         nc.sync.dma_start(table_list[:], offs)
-        nc.sync.dma_start(w4_codes[:].bitcast(I32), w4_words[0].bitcast(I32))
         nc.sync.dma_start(planes[1][:], x_planes[1])
 
         nc.scalar.dma_start(
@@ -82,7 +82,10 @@ def tile_list_htab_silu_kernel(tc, xT, w4_words, w4_scales, tab, u, wgt, b, offs
 
         cols = [slice(h * HALF, (h + 1) * HALF) for h in range(2)]
         list_cols = [slice(h * LIST_HALF, (h + 1) * LIST_HALF) for h in range(2)]
-        woven = [keep.tile([P, HALF, PACK], BF16, name="woven%d" % h, align_bytes=64) for h in range(2)]
+        woven = [
+            keep.tile([P, HALF, PACK], BF16, name="woven0", align_bytes=64, tag="woven0_then_codes1"),
+            keep.tile([P, HALF, PACK], BF16, name="woven1", align_bytes=64),
+        ]
 
         low = keep.tile([P, 2, S], F32, name="low")
         for i in range(2):
@@ -90,17 +93,20 @@ def tile_list_htab_silu_kernel(tc, xT, w4_words, w4_scales, tab, u, wgt, b, offs
         for h in range(2):
             nc.scalar.copy(woven[h][:, :, 0:2], low[:, :, cols[h]].rearrange("p i s -> p s i"))
 
-        picked_scales = keep.tile([P, S], U8, name="picked_scales")
+        picked_scales = keep.tile([P, S], U8, name="picked_scales", tag="picked_then_words")
         nc.vector.tensor_copy(picked_scales[:], table_scales[:].indirect(table_list[:]))
         nc.vector.tensor_copy(scale_planes[:].bitcast(I32)[:, : S // 4], picked_scales[:].bitcast(I32))
+        bias = keep.tile([P, P], F32, name="bias", align_bytes=64, tag="plane0_then_bias")
         nc.vector.transpose(bias[:], bias_rows[:])
-        table_words = keep.tile([P, T], I32, name="table_words", tag="scales_then_words")
-        nc.sync.dma_start(table_words[:], tab[0, 0 : 512 * T].rearrange("(p c) -> p c", p=P).bitcast(I32))
+        w4_codes = keep.tile([P, 2 * M], U8, name="w4_codes", align_bytes=64, tag="scales_then_w4")
+        nc.sync.dma_start(w4_codes[:].bitcast(I32), w4_words[0].bitcast(I32))
         for r in range(1, 4):
-            nc.scalar.dma_start(
+            nc.sync.dma_start(
                 scale_planes[:].bitcast(I32)[r:P:32, :],
                 scale_planes[:].bitcast(I32)[8 * r : P : 32, :],
             )
+        table_words = keep.tile([P, T], I32, name="table_words", tag="picked_then_words")
+        nc.sync.dma_start(table_words[:], tab[0, 0 : 512 * T].rearrange("(p c) -> p c", p=P).bitcast(I32))
 
         high = [keep.tile([P, 2, HALF], F32, name="high%d" % h) for h in range(2)]
         for i in range(2):
@@ -111,7 +117,10 @@ def tile_list_htab_silu_kernel(tc, xT, w4_words, w4_scales, tab, u, wgt, b, offs
         nc.scalar.copy(woven[0][:, :, 2:4], high[0][:].rearrange("p i s -> p s i"))
         nc.vector.tensor_copy(woven[1][:, :, 2:4], high[1][:].rearrange("p i s -> p s i"))
 
-        x_codes = [keep.tile([P, HALF], U32, name="x_codes%d" % h, align_bytes=64) for h in range(2)]
+        x_codes = [
+            keep.tile([P, HALF], U32, name="x_codes0", align_bytes=64),
+            keep.tile([P, HALF], U32, name="x_codes1", align_bytes=64, tag="woven0_then_codes1"),
+        ]
         x_scales = [keep.tile([P, HALF], U8, name="x_scales%d" % h, align_bytes=64) for h in range(2)]
         for h in range(2):
             nc.vector.quantize_mx(
@@ -132,22 +141,15 @@ def tile_list_htab_silu_kernel(tc, xT, w4_words, w4_scales, tab, u, wgt, b, offs
                         stop=False,
                     )
 
-        u_woven = [keep.tile([P, P, PACK], BF16, name="u_woven%d" % m, align_bytes=64) for m in range(M_TILES)]
-        u_codes = [keep.tile([P, P], U32, name="u_codes%d" % m, align_bytes=64) for m in range(M_TILES)]
-        u_scales = [keep.tile([P, P], U8, name="u_scales%d" % m, align_bytes=64) for m in range(M_TILES)]
-        u_views = [
-            (
-                u_woven[m][:].rearrange("p (c j) i -> p c i j", j=4),
-                u_rows[:, :, m * P : (m + 1) * P].rearrange("p i (c j) -> p c i j", j=4),
-            )
-            for m in range(M_TILES)
-        ]
-        nc.scalar.copy(*u_views[0])
-        nc.vector.tensor_copy(*u_views[1])
-        for m in range(M_TILES):
-            nc.vector.quantize_mx(
-                out=u_codes[m][:].bitcast(FP8X4), scales=u_scales[m][:], in_=u_woven[m][:].rearrange("p n i -> p (n i)")
-            )
+        u_woven = keep.tile([P, M, PACK], BF16, name="u_woven", align_bytes=64)
+        u_codes = keep.tile([P, M], U32, name="u_codes", align_bytes=64)
+        u_scales = keep.tile([P, M], U8, name="u_scales", align_bytes=64)
+        nc.scalar.copy(
+            u_woven[:].rearrange("p (c j) i -> p c i j", j=4), u_rows[:].rearrange("p i (c j) -> p c i j", j=4)
+        )
+        nc.vector.quantize_mx(
+            out=u_codes[:].bitcast(FP8X4), scales=u_scales[:], in_=u_woven[:].rearrange("p n i -> p (n i)")
+        )
 
         for h in range(2):
             picked_words = keep.tile([P, HALF], U32, name="picked_words%d" % h, align_bytes=64)
@@ -155,8 +157,8 @@ def tile_list_htab_silu_kernel(tc, xT, w4_words, w4_scales, tab, u, wgt, b, offs
             for m in range(M_TILES):
                 nc.tensor.matmul_mx(
                     out=banks[m][h][:],
-                    lhsT=u_codes[m][:].bitcast(FP8X4),
-                    lhsT_scale=u_scales[m][:],
+                    lhsT=u_codes[:, m * P : (m + 1) * P].bitcast(FP8X4),
+                    lhsT_scale=u_scales[:, m * P : (m + 1) * P],
                     rhs=picked_words[:].bitcast(FP8X4),
                     rhs_scale=scale_planes[:, cols[h]],
                     start=False,

@@ -46,7 +46,7 @@ def tile_list_htab_silu_kernel(tc, xT, w4_words, w4_scales, tab, u, wgt, b, offs
         nc.vector.memset(bias_rows[:], 0.0)
 
         x_planes = xT.rearrange("(p i) t -> i p t", i=PACK)
-        nc.sync.dma_start(folded[:], wgt[0:P:16, :].rearrange("g (c j) -> g c j", j=32))
+        nc.scalar.dma_start(folded[:], wgt[0:P:16, :].rearrange("g (c j) -> g c j", j=32))
         nc.sync.dma_start(planes[0][:], x_planes[0])
         nc.sync.dma_start(head_lists[:], offs2)
         nc.sync.dma_start(table_list[:], offs)
@@ -63,7 +63,7 @@ def tile_list_htab_silu_kernel(tc, xT, w4_words, w4_scales, tab, u, wgt, b, offs
         )
 
         turned = keep.tile([P, 32], F32, name="turned", align_bytes=64, tag="turned_then_plane3")
-        spread = keep.tile([P, S], F32, name="spread", align_bytes=64, tag="spread_then_u")
+        spread = keep.tile([P, S], F32, name="spread", align_bytes=64, tag="spread_then_u0")
         weights = keep.tile([P, S], F32, name="weights", align_bytes=64)
         nc.vector.transpose(turned[:], folded[:])
         nc.vector.tensor_copy(
@@ -75,10 +75,11 @@ def tile_list_htab_silu_kernel(tc, xT, w4_words, w4_scales, tab, u, wgt, b, offs
 
         planes.append(keep.tile([P, T], F32, name="plane2", align_bytes=64, tag="folded_then_plane2"))
         planes.append(keep.tile([P, T], F32, name="plane3", align_bytes=64, tag="turned_then_plane3"))
-        u_rows = keep.tile([P, PACK, M], F32, name="u_rows", align_bytes=64, tag="spread_then_u")
+        u_planes = u.rearrange("(p i) n -> p i n", i=PACK)
+        u_rows = [keep.tile([P, PACK, P], F32, name="u_rows0", align_bytes=64, tag="spread_then_u0")]
         for i in range(2, PACK):
             nc.sync.dma_start(planes[i][:], x_planes[i])
-        nc.sync.dma_start(u_rows[:], u.rearrange("(p i) n -> p i n", i=PACK))
+        nc.sync.dma_start(u_rows[0][:], u_planes[:, :, 0:P])
 
         cols = [slice(h * HALF, (h + 1) * HALF) for h in range(2)]
         list_cols = [slice(h * LIST_HALF, (h + 1) * LIST_HALF) for h in range(2)]
@@ -87,7 +88,7 @@ def tile_list_htab_silu_kernel(tc, xT, w4_words, w4_scales, tab, u, wgt, b, offs
             keep.tile([P, HALF, PACK], BF16, name="woven1", align_bytes=64),
         ]
 
-        low = keep.tile([P, 2, S], F32, name="low")
+        low = keep.tile([P, 2, S], F32, name="low", tag="low_then_u1_then_result")
         for i in range(2):
             nc.vector.tensor_tensor(low[:, i, :], planes[i][:].indirect(head_lists[:]), weights[:], MULT)
         for h in range(2):
@@ -107,6 +108,8 @@ def tile_list_htab_silu_kernel(tc, xT, w4_words, w4_scales, tab, u, wgt, b, offs
             )
         table_words = keep.tile([P, T], I32, name="table_words", tag="picked_then_words")
         nc.sync.dma_start(table_words[:], tab[0, 0 : 512 * T].rearrange("(p c) -> p c", p=P).bitcast(I32))
+        u_rows.append(keep.tile([P, PACK, P], F32, name="u_rows1", tag="low_then_u1_then_result"))
+        nc.sync.dma_start(u_rows[1][:], u_planes[:, :, P:M])
 
         high = [keep.tile([P, 2, HALF], F32, name="high%d" % h) for h in range(2)]
         for i in range(2):
@@ -141,29 +144,39 @@ def tile_list_htab_silu_kernel(tc, xT, w4_words, w4_scales, tab, u, wgt, b, offs
                         stop=False,
                     )
 
-        u_woven = keep.tile([P, M, PACK], BF16, name="u_woven", align_bytes=64)
-        u_codes = keep.tile([P, M], U32, name="u_codes", align_bytes=64)
-        u_scales = keep.tile([P, M], U8, name="u_scales", align_bytes=64)
-        nc.scalar.copy(
-            u_woven[:].rearrange("p (c j) i -> p c i j", j=4), u_rows[:].rearrange("p i (c j) -> p c i j", j=4)
-        )
-        nc.vector.quantize_mx(
-            out=u_codes[:].bitcast(FP8X4), scales=u_scales[:], in_=u_woven[:].rearrange("p n i -> p (n i)")
-        )
+        def quantise_u(m):
+            u_woven = keep.tile([P, P, PACK], BF16, name="u_woven%d" % m, align_bytes=64)
+            codes = keep.tile([P, P], U32, name="u_codes%d" % m, align_bytes=64)
+            scales = keep.tile([P, P], U8, name="u_scales%d" % m, align_bytes=64)
+            nc.scalar.copy(
+                u_woven[:].rearrange("p (c j) i -> p c i j", j=4), u_rows[m][:].rearrange("p i (c j) -> p c i j", j=4)
+            )
+            nc.vector.quantize_mx(
+                out=codes[:].bitcast(FP8X4), scales=scales[:], in_=u_woven[:].rearrange("p n i -> p (n i)")
+            )
+            return codes, scales
 
+        u_mx = [quantise_u(0)]
+        picked_words = [keep.tile([P, HALF], U32, name="picked_words%d" % h, align_bytes=64) for h in range(2)]
         for h in range(2):
-            picked_words = keep.tile([P, HALF], U32, name="picked_words%d" % h, align_bytes=64)
-            nc.vector.tensor_copy(picked_words[:], table_words[:].bitcast(U32).indirect(table_list[:, list_cols[h]]))
-            for m in range(M_TILES):
+            nc.vector.tensor_copy(
+                picked_words[h][:], table_words[:].bitcast(U32).indirect(table_list[:, list_cols[h]])
+            )
+        u_mx.append(quantise_u(1))
+
+        for m in range(M_TILES):
+            u_codes, u_scales = u_mx[m]
+            for h in range(2):
                 nc.tensor.matmul_mx(
                     out=banks[m][h][:],
-                    lhsT=u_codes[:, m * P : (m + 1) * P].bitcast(FP8X4),
-                    lhsT_scale=u_scales[:, m * P : (m + 1) * P],
-                    rhs=picked_words[:].bitcast(FP8X4),
+                    lhsT=u_codes[:].bitcast(FP8X4),
+                    lhsT_scale=u_scales[:],
+                    rhs=picked_words[h][:].bitcast(FP8X4),
                     rhs_scale=scale_planes[:, cols[h]],
                     start=False,
                     stop=True,
                 )
-                result = keep.tile([P, HALF], F32, name="result%d%d" % (m, h))
+                tag = "low_then_u1_then_result" if m + h == 0 else "result%d%d" % (m, h)
+                result = keep.tile([P, HALF], F32, name="result%d%d" % (m, h), tag=tag)
                 nc.scalar.activation(result[:], banks[m][h][:], SILU, bias=bias[:, 32 * m : 32 * m + 1])
                 nc.sync.dma_start(out[m * P : (m + 1) * P, cols[h]], result[:])

from contextlib import ExitStack

import concourse.mybir as mybir

K, L, M, T, S = 512, 512, 256, 2048, 512
FLOPS = 2 * (K + L) * M * S

F32 = mybir.dt.float32
BF16 = mybir.dt.bfloat16
I32 = mybir.dt.int32
U32 = mybir.dt.uint32
U16 = mybir.dt.uint16
U8 = mybir.dt.uint8
FP8X4 = mybir.dt.float8_e4m3fn_x4
FP4X4 = mybir.dt.float4_e2m1fn_x4
MULT = mybir.AluOpType.mult
SILU = mybir.ActivationFunctionType.Silu

P = 128
PACK = 4
HALF = S // 2
LIST_HALF = HALF // 16
M_TILES = M // P


def tile_list_htab_silu_kernel(tc, xT, w4_words, w4_scales, tab, u, wgt, b, offs, offs2, out):
    nc = tc.nc
    with ExitStack() as ctx:
        keep = ctx.enter_context(tc.tile_pool(name="keep", bufs=1))
        psum = ctx.enter_context(tc.psum_pool(name="psum", bufs=1))

        head_lists = keep.tile([P, S // 16], U16, name="head_lists")
        table_list = keep.tile([P, S // 16], U16, name="table_list")
        planes = [
            keep.tile([P, T], F32, name="plane0", align_bytes=64, tag="plane0_then_bias"),
            keep.tile([P, T], F32, name="plane1"),
        ]
        scale_planes = keep.tile([P, S + M], U8, name="scale_planes", align_bytes=64)
        bias_rows = keep.tile([P, P], F32, name="bias_rows", align_bytes=64)
        table_scales = keep.tile([P, T], U8, name="table_scales", align_bytes=64, tag="scales_then_w4")
        folded = keep.tile([P, 32], F32, name="folded", align_bytes=64, tag="folded_then_plane2")
        warm = keep.tile([P, 1], F32, name="warm")

        nc.vector.memset(table_scales[:].bitcast(I32), 0)
        nc.vector.memset(scale_planes[:].bitcast(I32)[:, S // 4 :], 0)
        nc.vector.memset(bias_rows[:], 0.0)

        x_planes = xT.rearrange("(p i) t -> i p t", i=PACK)
        nc.scalar.dma_start(folded[:], wgt[0:P:16, :].rearrange("g (c j) -> g c j", j=32))
        nc.sync.dma_start(planes[0][:], x_planes[0])
        nc.sync.dma_start(head_lists[:], offs2)
        nc.sync.dma_start(table_list[:], offs)
        nc.sync.dma_start(planes[1][:], x_planes[1])

        nc.scalar.dma_start(
            table_scales[:].bitcast(I32)[0:P:8, :],
            tab[0, 512 * T : 528 * T].rearrange("(q t) -> q t", q=16).bitcast(I32),
        )
        nc.scalar.dma_start(scale_planes[:].bitcast(I32)[0:P:8, S // 4 :], w4_scales[0].bitcast(I32))
        nc.scalar.dma_start(
            bias_rows[0:P:32, 0 : 32 * M_TILES].rearrange("q (m r) -> q m r", r=32),
            b.rearrange("(m q r) -> q m r", q=4, r=32),
        )

        turned = keep.tile([P, 32], F32, name="turned", align_bytes=64, tag="turned_then_plane3")
        spread = keep.tile([P, S], F32, name="spread", align_bytes=64, tag="spread_then_u0")
        weights = keep.tile([P, S], F32, name="weights", align_bytes=64)
        nc.vector.transpose(turned[:], folded[:])
        nc.vector.tensor_copy(
            spread[:].rearrange("p (c g r) -> p c g r", g=2, r=16),
            turned[:].rearrange("p (g c) -> p c g", g=2).unsqueeze(3).to_broadcast([P, 16, 2, 16]),
        )
        nc.vector.transpose(weights[:], spread[:])
        nc.scalar.activation(warm[:], weights[:, 0:1], SILU)

        planes.append(keep.tile([P, T], F32, name="plane2", align_bytes=64, tag="folded_then_plane2"))
        planes.append(keep.tile([P, T], F32, name="plane3", align_bytes=64, tag="turned_then_plane3"))
        u_planes = u.rearrange("(p i) n -> p i n", i=PACK)
        u_rows = [keep.tile([P, PACK, P], F32, name="u_rows0", align_bytes=64, tag="spread_then_u0")]
        for i in range(2, PACK):
            nc.sync.dma_start(planes[i][:], x_planes[i])
        nc.sync.dma_start(u_rows[0][:], u_planes[:, :, 0:P])

        cols = [slice(h * HALF, (h + 1) * HALF) for h in range(2)]
        list_cols = [slice(h * LIST_HALF, (h + 1) * LIST_HALF) for h in range(2)]
        woven = [
            keep.tile([P, HALF, PACK], BF16, name="woven0", align_bytes=64, tag="woven0_then_codes1"),
            keep.tile([P, HALF, PACK], BF16, name="woven1", align_bytes=64),
        ]

        low = keep.tile([P, 2, S], F32, name="low", tag="low_then_u1_then_result")
        for i in range(2):
            nc.vector.tensor_tensor(low[:, i, :], planes[i][:].indirect(head_lists[:]), weights[:], MULT)
        for h in range(2):
            nc.scalar.copy(woven[h][:, :, 0:2], low[:, :, cols[h]].rearrange("p i s -> p s i"))

        picked_scales = keep.tile([P, S], U8, name="picked_scales", tag="picked_then_words")
        nc.vector.tensor_copy(picked_scales[:], table_scales[:].indirect(table_list[:]))
        nc.vector.tensor_copy(scale_planes[:].bitcast(I32)[:, : S // 4], picked_scales[:].bitcast(I32))
        bias = keep.tile([P, P], F32, name="bias", align_bytes=64, tag="plane0_then_bias")
        nc.vector.transpose(bias[:], bias_rows[:])
        w4_codes = keep.tile([P, 2 * M], U8, name="w4_codes", align_bytes=64, tag="scales_then_w4")
        nc.sync.dma_start(w4_codes[:].bitcast(I32), w4_words[0].bitcast(I32))
        for r in range(1, 4):
            nc.sync.dma_start(
                scale_planes[:].bitcast(I32)[r:P:32, :],
                scale_planes[:].bitcast(I32)[8 * r : P : 32, :],
            )
        table_words = keep.tile([P, T], I32, name="table_words", tag="picked_then_words")
        nc.sync.dma_start(table_words[:], tab[0, 0 : 512 * T].rearrange("(p c) -> p c", p=P).bitcast(I32))
        u_rows.append(keep.tile([P, PACK, P], F32, name="u_rows1", tag="low_then_u1_then_result"))
        nc.sync.dma_start(u_rows[1][:], u_planes[:, :, P:M])

        high = [keep.tile([P, 2, HALF], F32, name="high%d" % h) for h in range(2)]
        for i in range(2):
            for h in range(2):
                nc.vector.tensor_tensor(
                    high[h][:, i, :], planes[2 + i][:].indirect(head_lists[:, list_cols[h]]), weights[:, cols[h]], MULT
                )
        nc.scalar.copy(woven[0][:, :, 2:4], high[0][:].rearrange("p i s -> p s i"))
        nc.vector.tensor_copy(woven[1][:, :, 2:4], high[1][:].rearrange("p i s -> p s i"))

        x_codes = [
            keep.tile([P, HALF], U32, name="x_codes0", align_bytes=64),
            keep.tile([P, HALF], U32, name="x_codes1", align_bytes=64, tag="woven0_then_codes1"),
        ]
        x_scales = [keep.tile([P, HALF], U8, name="x_scales%d" % h, align_bytes=64) for h in range(2)]
        for h in range(2):
            nc.vector.quantize_mx(
                out=x_codes[h][:].bitcast(FP8X4), scales=x_scales[h][:], in_=woven[h][:].rearrange("p s i -> p (s i)")
            )

        banks = [[psum.tile([P, HALF], F32, name="bank%d%d" % (m, h)) for h in range(2)] for m in range(M_TILES)]
        for h in range(2):
            for m in range(M_TILES):
                for n in range(HALF // P):
                    nc.tensor.matmul_mx(
                        out=banks[m][h][:, n * P : (n + 1) * P],
                        lhsT=w4_codes[:, 2 * m * P : 2 * (m + 1) * P].bitcast(FP4X4),
                        lhsT_scale=scale_planes[:, S + m * P : S + (m + 1) * P],
                        rhs=x_codes[h][:, n * P : (n + 1) * P].bitcast(FP8X4),
                        rhs_scale=x_scales[h][:, n * P : (n + 1) * P],
                        start=(n == 0),
                        stop=False,
                    )

        def quantise_u(m):
            u_woven = keep.tile([P, P, PACK], BF16, name="u_woven%d" % m, align_bytes=64)
            codes = keep.tile([P, P], U32, name="u_codes%d" % m, align_bytes=64)
            scales = keep.tile([P, P], U8, name="u_scales%d" % m, align_bytes=64)
            nc.scalar.copy(
                u_woven[:].rearrange("p (c j) i -> p c i j", j=4), u_rows[m][:].rearrange("p i (c j) -> p c i j", j=4)
            )
            nc.vector.quantize_mx(
                out=codes[:].bitcast(FP8X4), scales=scales[:], in_=u_woven[:].rearrange("p n i -> p (n i)")
            )
            return codes, scales

        u_mx = [quantise_u(0)]
        picked_words = [keep.tile([P, HALF], U32, name="picked_words%d" % h, align_bytes=64) for h in range(2)]
        for h in range(2):
            nc.vector.tensor_copy(
                picked_words[h][:], table_words[:].bitcast(U32).indirect(table_list[:, list_cols[h]])
            )
        u_mx.append(quantise_u(1))

        for m in range(M_TILES):
            u_codes, u_scales = u_mx[m]
            for h in range(2):
                nc.tensor.matmul_mx(
                    out=banks[m][h][:],
                    lhsT=u_codes[:].bitcast(FP8X4),
                    lhsT_scale=u_scales[:],
                    rhs=picked_words[h][:].bitcast(FP8X4),
                    rhs_scale=scale_planes[:, cols[h]],
                    start=False,
                    stop=True,
                )
                tag = "low_then_u1_then_result" if m + h == 0 else "result%d%d" % (m, h)
                result = keep.tile([P, HALF], F32, name="result%d%d" % (m, h), tag=tag)
                nc.scalar.activation(result[:], banks[m][h][:], SILU, bias=bias[:, 32 * m : 32 * m + 1])
                nc.sync.dma_start(out[m * P : (m + 1) * P, cols[h]], result[:])
